import numpy as np
CORES = [52,68,84,180,196,212,308,324,340]
N = 9
C, TIMES = 512, 2
def setup_inputs(rng):
    return {"x": np.exp(rng.standard_normal((N, 128, C), dtype=np.float32))}
def setup_inputs_big(rng):
    d = setup_inputs(rng)
    for k in ("x",): d[k] = (d[k].astype(np.float32) * 1048576.0).astype(d[k].dtype)
    return d
def setup_inputs_small(rng):
    d = setup_inputs(rng)
    for k in ("x",): d[k] = (d[k].astype(np.float32) * (1 / 1048576.0)).astype(d[k].dtype)
    return d
def setup_inputs_mixed(rng):
    d = setup_inputs(rng)
    f = (10.0 ** rng.uniform(-3, 3, (1, 1, C))).astype(np.float32)
    for k in ("x",): d[k] = (d[k].astype(np.float32) * f).astype(d[k].dtype)
    return d
def reference(x):
    X = x.astype(np.float64)
    for _ in range(TIMES):
        X = X / X.sum(axis=2, keepdims=True)
        X = X / X.sum(axis=(0, 1), keepdims=True)
    return {"y": X.astype(np.float32)}

@@ -1,0 +1,223 @@
+from concourse.bass import DstId, RemoteDMATransfer
+from concourse.mybir import AluOpType, AxisListType, ActivationFunctionType
+
+F = "float32"
+SCRATCH = {
+    "xs": ("sbuf", [128, 512], F), "xt": ("sbuf", [128, 512], F), "xu": ("sbuf", [128, 512], F),
+    "zu": ("sbuf", [128, 512], F), "zs": ("sbuf", [128, 512], F), "ys": ("sbuf", [128, 512], F),
+    "ones": ("sbuf", [128, 128], F), "ident": ("sbuf", [128, 128], F), "rmat": ("sbuf", [128, 128], F),
+    "ra": ("sbuf", [128, 32], F), "rb": ("sbuf", [128, 32], F),
+    "mask": ("sbuf", [128, 16], F),
+    "rs": ("sbuf", [128, 2], F), "rsum": ("sbuf", [128, 1], F), "r1": ("sbuf", [128, 1], F),
+    "part1": ("sbuf", [128, 4], F), "landH1": ("sbuf", [128, 8], F), "landL1": ("sbuf", [128, 24], F),
+    "tmp1": ("sbuf", [128, 4], F), "bufA1": ("sbuf", [128, 16], F), "bufB1": ("sbuf", [128, 8], F),
+    "c1": ("sbuf", [128, 4], F), "w1": ("sbuf", [128, 4], F),
+    "u1": ("sbuf", [128, 1], F), "urep": ("sbuf", [128, 4], F),
+    "part2": ("sbuf", [128, 16], F), "landH2": ("sbuf", [128, 32], F), "landL2": ("sbuf", [128, 96], F),
+    "tmp2": ("sbuf", [128, 16], F), "bufA2": ("sbuf", [128, 64], F), "bufB2": ("sbuf", [128, 32], F),
+    "tm": ("sbuf", [128, 16], F), "wv": ("sbuf", [128, 16], F),
+    "pc1": ("psum", [128, 512], F), "pt": ("psum", [128, 512], F), "ps": ("psum", [128, 512], F),
+    "pc2": ("psum", [128, 512], F), "pw": ("psum", [128, 512], F),
+}
+NLOCAL = 48
+SEMAPHORES = ["arrH1", "arrL1", "res1", "arrH2", "arrL2", "res2", "sent"] + ["l%d" % i for i in range(NLOCAL)]
+
+ADD, MUL = AluOpType.add, AluOpType.mult
+COPY = ActivationFunctionType.Copy
+
+
+def _plan(cores, topo):
+    hubs = [c for c in cores if all(topo.may_write(c, d) and topo.may_write(d, c) for d in cores if d != c)]
+    leaves = [c for c in cores if c not in hubs]
+    served = {h: [] for h in hubs}
+    for l in leaves:
+        h = sorted(hubs, key=lambda k: (len(served[k]), topo.chip(k) != topo.chip(l)))[0]
+        served[h].append(l)
+    return hubs, leaves, served
+
+
+def rank_program(g, core, T, topo):
+    if T.rank_of(core) is None:
+        return
+    hubs, leaves, served = _plan(list(T.cores), topo)
+    is_hub = core in hubs
+    V, A, P, S = g.vector, g.scalar, g.tensor, g.sync
+    used = [0]
+    sent = [0]
+
+    def sem():
+        used[0] += 1
+        return T.sem["l%d" % (used[0] - 1)]
+
+    def blk(t, q, w=128):
+        return t[:, q * w:(q + 1) * w]
+
+    def send(src, dests, dst_aps, rsem):
+        m = topo.mask(core, dests[0])
+        for d in dests:
+            m &= topo.mask(core, d)
+        ids = []
+        for d in dests:
+            rid, pid = topo.addr(d, core)
+            ids.append(DstId(rid=rid, pnc=pid))
+        g.remote_dma_fused([RemoteDMATransfer(dst_ids=ids, dma_engine_mask=m, remote_sem=rsem, srcs=[src],
+                                              dsts=dst_aps, alu_op=0)], local_sem=T.sem.sent)
+        sent[0] += bin(m).count("1")
+
+    def engines(src, dst):
+        return bin(topo.mask(src, dst)).count("1")
+
+    def send_part(part, landH, landL, wd, semH, semL):
+        dests = [h for h in hubs if h != core]
+        if is_hub:
+            aps = [blk(landH, [k for k in hubs if k != h].index(core), wd) for h in dests]
+            send(part[:], dests, aps, semH)
+        else:
+            send(part[:], dests, [blk(landL, leaves.index(core), wd)] * len(dests), semL)
+
+    def hub_sum(part, s_part, landH, landL, tmp, bufA, bufB, out, wd, semH, semL):
+        sa, sb, sc, sd = sem(), sem(), sem(), sem()
+        V.wait_ge(semH, sum(engines(h, core) for h in hubs if h != core))
+        V.wait_ge(s_part, 1)
+        V.tensor_tensor(tmp[:], landH[:, 0:wd], landH[:, wd:2 * wd], ADD).then_inc(sa, 1)
+        V.wait_ge(sa, 1)
+        V.tensor_tensor(bufA[:, 3 * wd:4 * wd], tmp[:], part[:], ADD).then_inc(sb, 1)
+        V.wait_ge(semL, sum(engines(l, core) for l in leaves))
+        V.tensor_tensor(bufA[:, 0:3 * wd], landL[:, 0:3 * wd], landL[:, 3 * wd:6 * wd], ADD).then_inc(sb, 1)
+        V.wait_ge(sb, 2)
+        V.tensor_tensor(bufB[:], bufA[:, 0:2 * wd], bufA[:, 2 * wd:4 * wd], ADD).then_inc(sc, 1)
+        V.wait_ge(sc, 1)
+        V.tensor_tensor(out[:], bufB[:, 0:wd], bufB[:, wd:2 * wd], ADD).then_inc(sd, 1)
+        return sd
+
+    ld = sem()
+    S.dma_start(T.xs[:], T.x[:]).then_inc(ld, 16)
+    c_ones, c_id, m0, m1 = sem(), sem(), sem(), sem()
+    V.memset(T.ones[:], 1.0).then_inc(c_ones, 1)
+    g.wait_ge(c_ones, 1)
+    g.affine_select(T.ident[:], T.ones[:], [[-1, 128]], AluOpType.is_equal, 0.0, 0, 1).then_inc(c_id, 1)
+    V.memset(T.mask[:], 0.0).then_inc(m0, 1)
+    V.wait_ge(m0, 1)
+    for a in range(4):
+        V.memset(T.mask[32 * a:32 * a + 32, a:16:4], 1.0).then_inc(m1, 1)
+    V.wait_ge(c_ones, 1)
+    c_r = None
+    if is_hub:
+        q0, q1, q2, c_r = sem(), sem(), sem(), sem()
+        V.wait_ge(c_id, 1)
+        V.tensor_tensor(T.ra[:], T.ident[:, 0:32], T.ident[:, 32:64], ADD).then_inc(q0, 1)
+        V.tensor_tensor(T.rb[:], T.ident[:, 64:96], T.ident[:, 96:128], ADD).then_inc(q0, 1)
+        V.wait_ge(q0, 2)
+        V.tensor_tensor(T.rmat[:, 0:32], T.ra[:], T.rb[:], ADD).then_inc(q1, 1)
+        V.wait_ge(q1, 1)
+        V.tensor_copy(T.rmat[:, 32:64], T.rmat[:, 0:32]).then_inc(q2, 1)
+        V.wait_ge(q2, 1)
+        V.tensor_copy(T.rmat[:, 64:128], T.rmat[:, 0:64]).then_inc(c_r, 1)
+
+    s_rs, s_rsum, s_r1, s_pc1, s_part1 = sem(), sem(), sem(), sem(), sem()
+    V.wait_ge(ld, 16)
+    V.tensor_reduce(T.rs[:, 0:1], T.xs[:, 0:256], AxisListType.X, ADD).then_inc(s_rs, 1)
+    A.wait_ge(ld, 16)
+    A.activation(T.ys[:, 0:256], T.xs[:, 256:512], COPY, accum_out=T.rs[:, 1:2]).then_inc(s_rs, 1)
+    V.wait_ge(s_rs, 2)
+    V.tensor_tensor(T.rsum[:], T.rs[:, 0:1], T.rs[:, 1:2], ADD).then_inc(s_rsum, 1)
+    V.wait_ge(s_rsum, 1)
+    V.reciprocal(T.r1[:], T.rsum[:]).then_inc(s_r1, 1)
+    P.wait_ge(ld, 16)
+    P.wait_ge(s_r1, 1)
+    for q in range(4):
+        P.matmul(T.pc1[:, q:q + 1], blk(T.xs, q), T.r1[:], True, True).then_inc(s_pc1, 1)
+    V.wait_ge(s_pc1, 4)
+    V.tensor_copy(T.part1[:], T.pc1[:, 0:4]).then_inc(s_part1, 1)
+    g.wait_ge(s_part1, 1)
+    send_part(T.part1, T.landH1, T.landL1, 4, T.sem.arrH1, T.sem.arrL1)
+
+    s_pt, s_xt = sem(), sem()
+    P.wait_ge(c_id, 1)
+    for q in range(4):
+        P.transpose(blk(T.pt, q), blk(T.xs, q), T.ident[:]).then_inc(s_pt, 1)
+    A.wait_ge(s_pt, 4)
+    A.activation(T.xt[:], T.pt[:], COPY).then_inc(s_xt, 1)
+
+    if is_hub:
+        s_c1 = hub_sum(T.part1, s_part1, T.landH1, T.landL1, T.tmp1, T.bufA1, T.bufB1, T.c1, 4,
+                       T.sem.arrH1, T.sem.arrL1)
+        s_w1, n_w1 = sem(), 1
+        V.wait_ge(s_c1, 1)
+        V.reciprocal(T.w1[:], T.c1[:]).then_inc(s_w1, 1)
+        g.wait_ge(s_w1, 1)
+        send(T.w1[:], served[core], [T.w1[:]] * len(served[core]), T.sem.res1)
+    else:
+        my_hub = [h for h in hubs if core in served[h]][0]
+        s_w1, n_w1 = T.sem.res1, engines(my_hub, core)
+
+    s_ps, s_u1, s_u, s_pc2, s_part2 = sem(), sem(), sem(), sem(), sem()
+    P.wait_ge(s_w1, n_w1)
+    P.wait_ge(s_xt, 1)
+    for q in range(4):
+        P.matmul(T.ps[:, 0:1], blk(T.xt, q), T.w1[:, q:q + 1], q == 0, q == 3).then_inc(s_ps, 1)
+    V.wait_ge(s_ps, 4)
+    V.reciprocal(T.u1[:], T.ps[:, 0:1]).then_inc(s_u1, 1)
+    V.wait_ge(s_u1, 1)
+    V.tensor_scalar(T.urep[:], T.ones[:, 0:4], T.u1[:, 0:1], None, MUL).then_inc(s_u, 1)
+    P.wait_ge(s_u, 1)
+    for q in range(4):
+        P.matmul(blk(T.pc2, q, 4), blk(T.xs, q), T.urep[:], True, True).then_inc(s_pc2, 1)
+    V.wait_ge(s_pc2, 4)
+    V.wait_ge(m1, 4)
+    V.tensor_tensor(T.part2[:], T.pc2[:, 0:16], T.mask[:], MUL).then_inc(s_part2, 1)
+    g.wait_ge(s_part2, 1)
+    send_part(T.part2, T.landH2, T.landL2, 16, T.sem.arrH2, T.sem.arrL2)
+
+    s_xu, s_zu = sem(), sem()
+    A.wait_ge(s_u, 1)
+    A.activation(T.xu[:], T.xs[:], COPY, scale=T.urep[:, 0:1]).then_inc(s_xu, 1)
+    V.wait_ge(s_xu, 1)
+    V.transpose(T.zu[:], T.xu[:]).then_inc(s_zu, 1)
+
+    if is_hub:
+        s_tm = hub_sum(T.part2, s_part2, T.landH2, T.landL2, T.tmp2, T.bufA2, T.bufB2, T.tm, 16,
+                       T.sem.arrH2, T.sem.arrL2)
+        s_pw, s_wv, n_wv = sem(), sem(), 1
+        P.wait_ge(c_r, 1)
+        P.wait_ge(s_tm, 1)
+        P.matmul(T.pw[:, 0:16], T.rmat[:], T.tm[:], True, True).then_inc(s_pw, 1)
+        V.wait_ge(s_pw, 1)
+        V.reciprocal(T.wv[:], T.pw[:, 0:16]).then_inc(s_wv, 1)
+        g.wait_ge(s_wv, 1)
+        send(T.wv[:], served[core], [T.wv[:]] * len(served[core]), T.sem.res2)
+    else:
+        s_wv, n_wv = T.sem.res2, engines(my_hub, core)
+
+    s_z = [sem() for _ in range(4)]
+    s_y = [sem() for _ in range(2)]
+    st = sem()
+    A.wait_ge(s_wv, n_wv)
+    A.wait_ge(s_zu, 1)
+    for b in range(16):
+        if b % 4 != 3:
+            A.activation(blk(T.zs, b, 32), blk(T.zu, b, 32), COPY, scale=T.wv[:, b:b + 1]).then_inc(s_z[b // 4], 1)
+
+    def vscale(q):
+        b = 4 * q + 3
+        V.tensor_scalar(blk(T.zs, b, 32), blk(T.zu, b, 32), T.wv[:, b:b + 1], None, MUL).then_inc(s_z[q], 1)
+
+    def vback(q):
+        V.wait_ge(s_z[q], 4)
+        V.transpose(blk(T.ys, q), blk(T.zs, q)).then_inc(s_y[q // 2], 1)
+
+    V.wait_ge(s_wv, n_wv)
+    V.wait_ge(s_zu, 1)
+    vscale(0)
+    vscale(1)
+    vback(0)
+    vscale(2)
+    vback(1)
+    vscale(3)
+    vback(2)
+    vback(3)
+    for h in range(2):
+        S.wait_ge(s_y[h], 2)
+        S.dma_start(T.y[:, 256 * h:256 * h + 256], T.ys[:, 256 * h:256 * h + 256]).then_inc(st, 16)
+    S.wait_ge(st, 32)
+    g.wait_ge(T.sem.sent, sent[0])

@@ -2,25 +2,23 @@ from concourse.bass import DstId, RemoteDMATransfer
 from concourse.mybir import AluOpType, AxisListType, ActivationFunctionType
 
 F = "float32"
+NR = 9
 SCRATCH = {
     "xs": ("sbuf", [128, 512], F), "xt": ("sbuf", [128, 512], F), "xu": ("sbuf", [128, 512], F),
     "zu": ("sbuf", [128, 512], F), "zs": ("sbuf", [128, 512], F), "ys": ("sbuf", [128, 512], F),
     "ones": ("sbuf", [128, 128], F), "ident": ("sbuf", [128, 128], F), "rmat": ("sbuf", [128, 128], F),
     "ra": ("sbuf", [128, 32], F), "rb": ("sbuf", [128, 32], F),
-    "mask": ("sbuf", [128, 16], F),
+    "ind": ("sbuf", [128, 4], F),
     "rs": ("sbuf", [128, 2], F), "rsum": ("sbuf", [128, 1], F), "r1": ("sbuf", [128, 1], F),
-    "part1": ("sbuf", [128, 4], F), "landH1": ("sbuf", [128, 8], F), "landL1": ("sbuf", [128, 24], F),
-    "tmp1": ("sbuf", [128, 4], F), "bufA1": ("sbuf", [128, 16], F), "bufB1": ("sbuf", [128, 8], F),
-    "c1": ("sbuf", [128, 4], F), "w1": ("sbuf", [128, 4], F),
-    "u1": ("sbuf", [128, 1], F), "urep": ("sbuf", [128, 4], F),
-    "part2": ("sbuf", [128, 16], F), "landH2": ("sbuf", [128, 32], F), "landL2": ("sbuf", [128, 96], F),
-    "tmp2": ("sbuf", [128, 16], F), "bufA2": ("sbuf", [128, 64], F), "bufB2": ("sbuf", [128, 32], F),
+    "land1": ("sbuf", [128, 4 * NR], F), "c1": ("sbuf", [128, 4], F), "w1": ("sbuf", [128, 4], F),
+    "u1": ("sbuf", [128, 1], F),
+    "land2": ("sbuf", [128, 4 * NR], F), "t4": ("sbuf", [128, 4], F),
     "tm": ("sbuf", [128, 16], F), "wv": ("sbuf", [128, 16], F),
     "pc1": ("psum", [128, 512], F), "pt": ("psum", [128, 512], F), "ps": ("psum", [128, 512], F),
     "pc2": ("psum", [128, 512], F), "pw": ("psum", [128, 512], F),
 }
 NLOCAL = 48
-SEMAPHORES = ["arrH1", "arrL1", "res1", "arrH2", "arrL2", "res2", "sent"] + ["l%d" % i for i in range(NLOCAL)]
+SEMAPHORES = ["arr1", "res1", "arr2", "res2", "sent"] + ["l%d" % i for i in range(NLOCAL)]
 
 ADD, MUL = AluOpType.add, AluOpType.mult
 COPY = ActivationFunctionType.Copy
@@ -39,8 +37,10 @@ def _plan(cores, topo):
 def rank_program(g, core, T, topo):
     if T.rank_of(core) is None:
         return
-    hubs, leaves, served = _plan(list(T.cores), topo)
+    cores = list(T.cores)
+    hubs, leaves, served = _plan(cores, topo)
     is_hub = core in hubs
+    me = cores.index(core)
     V, A, P, S = g.vector, g.scalar, g.tensor, g.sync
     used = [0]
     sent = [0]
@@ -67,27 +67,18 @@ def rank_program(g, core, T, topo):
     def engines(src, dst):
         return bin(topo.mask(src, dst)).count("1")
 
-    def send_part(part, landH, landL, wd, semH, semL):
-        dests = [h for h in hubs if h != core]
-        if is_hub:
-            aps = [blk(landH, [k for k in hubs if k != h].index(core), wd) for h in dests]
-            send(part[:], dests, aps, semH)
-        else:
-            send(part[:], dests, [blk(landL, leaves.index(core), wd)] * len(dests), semL)
+    n_in = sum(engines(c, core) for c in cores if c != core)
 
-    def hub_sum(part, s_part, landH, landL, tmp, bufA, bufB, out, wd, semH, semL):
-        sa, sb, sc, sd = sem(), sem(), sem(), sem()
-        V.wait_ge(semH, sum(engines(h, core) for h in hubs if h != core))
+    def send_part(land, arr):
+        dests = [h for h in hubs if h != core]
+        send(blk(land, me, 4), dests, [blk(land, me, 4)] * len(dests), arr)
+
+    def hub_sum(land, s_part, out, arr):
+        sd = sem()
         V.wait_ge(s_part, 1)
-        V.tensor_tensor(tmp[:], landH[:, 0:wd], landH[:, wd:2 * wd], ADD).then_inc(sa, 1)
-        V.wait_ge(sa, 1)
-        V.tensor_tensor(bufA[:, 3 * wd:4 * wd], tmp[:], part[:], ADD).then_inc(sb, 1)
-        V.wait_ge(semL, sum(engines(l, core) for l in leaves))
-        V.tensor_tensor(bufA[:, 0:3 * wd], landL[:, 0:3 * wd], landL[:, 3 * wd:6 * wd], ADD).then_inc(sb, 1)
-        V.wait_ge(sb, 2)
-        V.tensor_tensor(bufB[:], bufA[:, 0:2 * wd], bufA[:, 2 * wd:4 * wd], ADD).then_inc(sc, 1)
-        V.wait_ge(sc, 1)
-        V.tensor_tensor(out[:], bufB[:, 0:wd], bufB[:, wd:2 * wd], ADD).then_inc(sd, 1)
+        V.wait_ge(arr, n_in)
+        for q in range(4):
+            V.tensor_reduce(out[:, q:q + 1], land[:, q:4 * NR:4], AxisListType.X, ADD).then_inc(sd, 1)
         return sd
 
     ld = sem()
@@ -96,23 +87,10 @@ def rank_program(g, core, T, topo):
     V.memset(T.ones[:], 1.0).then_inc(c_ones, 1)
     g.wait_ge(c_ones, 1)
     g.affine_select(T.ident[:], T.ones[:], [[-1, 128]], AluOpType.is_equal, 0.0, 0, 1).then_inc(c_id, 1)
-    V.memset(T.mask[:], 0.0).then_inc(m0, 1)
+    V.memset(T.ind[:], 0.0).then_inc(m0, 1)
     V.wait_ge(m0, 1)
     for a in range(4):
-        V.memset(T.mask[32 * a:32 * a + 32, a:16:4], 1.0).then_inc(m1, 1)
-    V.wait_ge(c_ones, 1)
-    c_r = None
-    if is_hub:
-        q0, q1, q2, c_r = sem(), sem(), sem(), sem()
-        V.wait_ge(c_id, 1)
-        V.tensor_tensor(T.ra[:], T.ident[:, 0:32], T.ident[:, 32:64], ADD).then_inc(q0, 1)
-        V.tensor_tensor(T.rb[:], T.ident[:, 64:96], T.ident[:, 96:128], ADD).then_inc(q0, 1)
-        V.wait_ge(q0, 2)
-        V.tensor_tensor(T.rmat[:, 0:32], T.ra[:], T.rb[:], ADD).then_inc(q1, 1)
-        V.wait_ge(q1, 1)
-        V.tensor_copy(T.rmat[:, 32:64], T.rmat[:, 0:32]).then_inc(q2, 1)
-        V.wait_ge(q2, 1)
-        V.tensor_copy(T.rmat[:, 64:128], T.rmat[:, 0:64]).then_inc(c_r, 1)
+        V.memset(T.ind[32 * a:32 * a + 32, a:a + 1], 1.0).then_inc(m1, 1)
 
     s_rs, s_rsum, s_r1, s_pc1, s_part1 = sem(), sem(), sem(), sem(), sem()
     V.wait_ge(ld, 16)
@@ -128,9 +106,20 @@ def rank_program(g, core, T, topo):
     for q in range(4):
         P.matmul(T.pc1[:, q:q + 1], blk(T.xs, q), T.r1[:], True, True).then_inc(s_pc1, 1)
     V.wait_ge(s_pc1, 4)
-    V.tensor_copy(T.part1[:], T.pc1[:, 0:4]).then_inc(s_part1, 1)
+    V.tensor_copy(blk(T.land1, me, 4), T.pc1[:, 0:4]).then_inc(s_part1, 1)
     g.wait_ge(s_part1, 1)
-    send_part(T.part1, T.landH1, T.landL1, 4, T.sem.arrH1, T.sem.arrL1)
+    send_part(T.land1, T.sem.arr1)
+
+    q0, q1, q2, c_r = sem(), sem(), sem(), sem()
+    V.wait_ge(c_id, 1)
+    V.tensor_tensor(T.ra[:], T.ident[:, 0:32], T.ident[:, 32:64], ADD).then_inc(q0, 1)
+    V.tensor_tensor(T.rb[:], T.ident[:, 64:96], T.ident[:, 96:128], ADD).then_inc(q0, 1)
+    V.wait_ge(q0, 2)
+    V.tensor_tensor(T.rmat[:, 0:32], T.ra[:], T.rb[:], ADD).then_inc(q1, 1)
+    V.wait_ge(q1, 1)
+    V.tensor_copy(T.rmat[:, 32:64], T.rmat[:, 0:32]).then_inc(q2, 1)
+    V.wait_ge(q2, 1)
+    V.tensor_copy(T.rmat[:, 64:128], T.rmat[:, 0:64]).then_inc(c_r, 1)
 
     s_pt, s_xt = sem(), sem()
     P.wait_ge(c_id, 1)
@@ -140,10 +129,9 @@ def rank_program(g, core, T, topo):
     A.activation(T.xt[:], T.pt[:], COPY).then_inc(s_xt, 1)
 
     if is_hub:
-        s_c1 = hub_sum(T.part1, s_part1, T.landH1, T.landL1, T.tmp1, T.bufA1, T.bufB1, T.c1, 4,
-                       T.sem.arrH1, T.sem.arrL1)
+        s_c1 = hub_sum(T.land1, s_part1, T.c1, T.sem.arr1)
         s_w1, n_w1 = sem(), 1
-        V.wait_ge(s_c1, 1)
+        V.wait_ge(s_c1, 4)
         V.reciprocal(T.w1[:], T.c1[:]).then_inc(s_w1, 1)
         g.wait_ge(s_w1, 1)
         send(T.w1[:], served[core], [T.w1[:]] * len(served[core]), T.sem.res1)
@@ -151,62 +139,71 @@ def rank_program(g, core, T, topo):
         my_hub = [h for h in hubs if core in served[h]][0]
         s_w1, n_w1 = T.sem.res1, engines(my_hub, core)
 
-    s_ps, s_u1, s_u, s_pc2, s_part2 = sem(), sem(), sem(), sem(), sem()
+    s_ps, s_u1, s_pc2, s_part2 = sem(), sem(), sem(), sem()
     P.wait_ge(s_w1, n_w1)
     P.wait_ge(s_xt, 1)
     for q in range(4):
         P.matmul(T.ps[:, 0:1], blk(T.xt, q), T.w1[:, q:q + 1], q == 0, q == 3).then_inc(s_ps, 1)
     V.wait_ge(s_ps, 4)
     V.reciprocal(T.u1[:], T.ps[:, 0:1]).then_inc(s_u1, 1)
-    V.wait_ge(s_u1, 1)
-    V.tensor_scalar(T.urep[:], T.ones[:, 0:4], T.u1[:, 0:1], None, MUL).then_inc(s_u, 1)
-    P.wait_ge(s_u, 1)
+    P.wait_ge(s_u1, 1)
     for q in range(4):
-        P.matmul(blk(T.pc2, q, 4), blk(T.xs, q), T.urep[:], True, True).then_inc(s_pc2, 1)
+        P.matmul(T.pc2[:, q:q + 1], blk(T.xs, q), T.u1[:], True, True).then_inc(s_pc2, 1)
     V.wait_ge(s_pc2, 4)
-    V.wait_ge(m1, 4)
-    V.tensor_tensor(T.part2[:], T.pc2[:, 0:16], T.mask[:], MUL).then_inc(s_part2, 1)
+    V.tensor_copy(blk(T.land2, me, 4), T.pc2[:, 0:4]).then_inc(s_part2, 1)
     g.wait_ge(s_part2, 1)
-    send_part(T.part2, T.landH2, T.landL2, 16, T.sem.arrH2, T.sem.arrL2)
+    send_part(T.land2, T.sem.arr2)
 
     s_xu, s_zu = sem(), sem()
-    A.wait_ge(s_u, 1)
-    A.activation(T.xu[:], T.xs[:], COPY, scale=T.urep[:, 0:1]).then_inc(s_xu, 1)
+    A.wait_ge(s_u1, 1)
+    A.activation(T.xu[:], T.xs[:], COPY, scale=T.u1[:, 0:1]).then_inc(s_xu, 1)
     V.wait_ge(s_xu, 1)
     V.transpose(T.zu[:], T.xu[:]).then_inc(s_zu, 1)
 
     if is_hub:
-        s_tm = hub_sum(T.part2, s_part2, T.landH2, T.landL2, T.tmp2, T.bufA2, T.bufB2, T.tm, 16,
-                       T.sem.arrH2, T.sem.arrL2)
-        s_pw, s_wv, n_wv = sem(), sem(), 1
-        P.wait_ge(c_r, 1)
-        P.wait_ge(s_tm, 1)
-        P.matmul(T.pw[:, 0:16], T.rmat[:], T.tm[:], True, True).then_inc(s_pw, 1)
-        V.wait_ge(s_pw, 1)
-        V.reciprocal(T.wv[:], T.pw[:, 0:16]).then_inc(s_wv, 1)
-        g.wait_ge(s_wv, 1)
-        send(T.wv[:], served[core], [T.wv[:]] * len(served[core]), T.sem.res2)
+        s_t, n_t = hub_sum(T.land2, s_part2, T.t4, T.sem.arr2), 4
+        g.wait_ge(s_t, n_t)
+        send(T.t4[:], served[core], [T.t4[:]] * len(served[core]), T.sem.res2)
     else:
-        s_wv, n_wv = T.sem.res2, engines(my_hub, core)
+        s_t, n_t = T.sem.res2, engines(my_hub, core)
+
+    s_tm, s_pw, s_wv = sem(), sem(), sem()
+    V.wait_ge(m1, 4)
+    V.wait_ge(s_t, n_t)
+    A.wait_ge(m1, 4)
+    A.wait_ge(s_t, n_t)
+    for a in range(2):
+        V.tensor_scalar(blk(T.tm, a, 4), T.t4[:], T.ind[:, a:a + 1], None, MUL).then_inc(s_tm, 1)
+    for a in range(2, 4):
+        A.activation(blk(T.tm, a, 4), T.t4[:], COPY, scale=T.ind[:, a:a + 1]).then_inc(s_tm, 1)
+    P.wait_ge(c_r, 1)
+    P.wait_ge(s_tm, 4)
+    P.matmul(T.pw[:, 0:16], T.rmat[:], T.tm[:], True, True).then_inc(s_pw, 1)
+    V.wait_ge(s_pw, 1)
+    V.reciprocal(T.wv[:], T.pw[:, 0:16]).then_inc(s_wv, 1)
+
+    def col(b):
+        c = 4 * (b % 4) + b // 4
+        return T.wv[:, c:c + 1]
 
     s_z = [sem() for _ in range(4)]
     s_y = [sem() for _ in range(2)]
     st = sem()
-    A.wait_ge(s_wv, n_wv)
+    A.wait_ge(s_wv, 1)
     A.wait_ge(s_zu, 1)
     for b in range(16):
         if b % 4 != 3:
-            A.activation(blk(T.zs, b, 32), blk(T.zu, b, 32), COPY, scale=T.wv[:, b:b + 1]).then_inc(s_z[b // 4], 1)
+            A.activation(blk(T.zs, b, 32), blk(T.zu, b, 32), COPY, scale=col(b)).then_inc(s_z[b // 4], 1)
 
     def vscale(q):
         b = 4 * q + 3
-        V.tensor_scalar(blk(T.zs, b, 32), blk(T.zu, b, 32), T.wv[:, b:b + 1], None, MUL).then_inc(s_z[q], 1)
+        V.tensor_scalar(blk(T.zs, b, 32), blk(T.zu, b, 32), col(b), None, MUL).then_inc(s_z[q], 1)
 
     def vback(q):
         V.wait_ge(s_z[q], 4)
         V.transpose(blk(T.ys, q), blk(T.zs, q)).then_inc(s_y[q // 2], 1)
 
-    V.wait_ge(s_wv, n_wv)
+    V.wait_ge(s_wv, 1)
     V.wait_ge(s_zu, 1)
     vscale(0)
     vscale(1)

@@ -4,18 +4,18 @@ from concourse.mybir import AluOpType, AxisListType, ActivationFunctionType
 F = "float32"
 NR = 9
 SCRATCH = {
-    "xs": ("sbuf", [128, 512], F), "xt": ("sbuf", [128, 512], F), "xu": ("sbuf", [128, 512], F),
-    "zu": ("sbuf", [128, 512], F), "zs": ("sbuf", [128, 512], F), "ys": ("sbuf", [128, 512], F),
-    "ones": ("sbuf", [128, 128], F), "ident": ("sbuf", [128, 128], F), "rmat": ("sbuf", [128, 128], F),
-    "ra": ("sbuf", [128, 32], F), "rb": ("sbuf", [128, 32], F),
-    "ind": ("sbuf", [128, 4], F),
-    "rs": ("sbuf", [128, 2], F), "rsum": ("sbuf", [128, 1], F), "r1": ("sbuf", [128, 1], F),
+    "xs": ("sbuf", [128, 512], F), "xt": ("sbuf", [128, 512], F), "xq": ("sbuf", [128, 512], F),
+    "zs": ("sbuf", [128, 512], F), "ys": ("sbuf", [128, 512], F), "sc": ("sbuf", [128, 256], F),
+    "ones": ("sbuf", [128, 128], F), "ident": ("sbuf", [128, 128], F), "pmat": ("sbuf", [128, 128], F),
+    "pu": ("sbuf", [128, 128], F),
+    "r1": ("sbuf", [128, 1], F),
     "land1": ("sbuf", [128, 4 * NR], F), "c1": ("sbuf", [128, 4], F), "w1": ("sbuf", [128, 4], F),
     "u1": ("sbuf", [128, 1], F),
-    "land2": ("sbuf", [128, 4 * NR], F), "t4": ("sbuf", [128, 4], F),
-    "tm": ("sbuf", [128, 16], F), "wv": ("sbuf", [128, 16], F),
+    "land2": ("sbuf", [128, 4 * NR], F), "t4": ("sbuf", [128, 4], F), "v4": ("sbuf", [128, 4], F),
     "pc1": ("psum", [128, 512], F), "pt": ("psum", [128, 512], F), "ps": ("psum", [128, 512], F),
-    "pc2": ("psum", [128, 512], F), "pw": ("psum", [128, 512], F),
+    "pc2": ("psum", [128, 512], F),
+    "z0": ("psum", [128, 512], F), "z1": ("psum", [128, 512], F), "z2": ("psum", [128, 512], F),
+    "z3": ("psum", [128, 512], F),
 }
 NLOCAL = 48
 SEMAPHORES = ["arr1", "res1", "arr2", "res2", "sent"] + ["l%d" % i for i in range(NLOCAL)]
@@ -83,24 +83,18 @@ def rank_program(g, core, T, topo):
 
     ld = sem()
     S.dma_start(T.xs[:], T.x[:]).then_inc(ld, 16)
-    c_ones, c_id, m0, m1 = sem(), sem(), sem(), sem()
+    c_ones, c_id, c_perm = sem(), sem(), sem()
     V.memset(T.ones[:], 1.0).then_inc(c_ones, 1)
     g.wait_ge(c_ones, 1)
     g.affine_select(T.ident[:], T.ones[:], [[-1, 128]], AluOpType.is_equal, 0.0, 0, 1).then_inc(c_id, 1)
-    V.memset(T.ind[:], 0.0).then_inc(m0, 1)
-    V.wait_ge(m0, 1)
-    for a in range(4):
-        V.memset(T.ind[32 * a:32 * a + 32, a:a + 1], 1.0).then_inc(m1, 1)
+    g.affine_select(T.pmat[:], T.ones[:], [[-64, 2], [-1, 2], [-2, 32]], AluOpType.is_equal, 0.0, 0,
+                    1).then_inc(c_perm, 1)
 
-    s_rs, s_rsum, s_r1, s_pc1, s_part1 = sem(), sem(), sem(), sem(), sem()
+    s_rs, s_r1, s_pc1, s_part1 = sem(), sem(), sem(), sem()
     V.wait_ge(ld, 16)
-    V.tensor_reduce(T.rs[:, 0:1], T.xs[:, 0:256], AxisListType.X, ADD).then_inc(s_rs, 1)
-    A.wait_ge(ld, 16)
-    A.activation(T.ys[:, 0:256], T.xs[:, 256:512], COPY, accum_out=T.rs[:, 1:2]).then_inc(s_rs, 1)
-    V.wait_ge(s_rs, 2)
-    V.tensor_tensor(T.rsum[:], T.rs[:, 0:1], T.rs[:, 1:2], ADD).then_inc(s_rsum, 1)
-    V.wait_ge(s_rsum, 1)
-    V.reciprocal(T.r1[:], T.rsum[:]).then_inc(s_r1, 1)
+    V.tensor_tensor_scan(T.sc[:], T.xs[:, 0:256], T.xs[:, 256:512], 0.0, ADD, ADD).then_inc(s_rs, 1)
+    V.wait_ge(s_rs, 1)
+    V.reciprocal(T.r1[:], T.sc[:, 255:256]).then_inc(s_r1, 1)
     P.wait_ge(ld, 16)
     P.wait_ge(s_r1, 1)
     for q in range(4):
@@ -110,16 +104,10 @@ def rank_program(g, core, T, topo):
     g.wait_ge(s_part1, 1)
     send_part(T.land1, T.sem.arr1)
 
-    q0, q1, q2, c_r = sem(), sem(), sem(), sem()
-    V.wait_ge(c_id, 1)
-    V.tensor_tensor(T.ra[:], T.ident[:, 0:32], T.ident[:, 32:64], ADD).then_inc(q0, 1)
-    V.tensor_tensor(T.rb[:], T.ident[:, 64:96], T.ident[:, 96:128], ADD).then_inc(q0, 1)
-    V.wait_ge(q0, 2)
-    V.tensor_tensor(T.rmat[:, 0:32], T.ra[:], T.rb[:], ADD).then_inc(q1, 1)
-    V.wait_ge(q1, 1)
-    V.tensor_copy(T.rmat[:, 32:64], T.rmat[:, 0:32]).then_inc(q2, 1)
-    V.wait_ge(q2, 1)
-    V.tensor_copy(T.rmat[:, 64:128], T.rmat[:, 0:64]).then_inc(c_r, 1)
+    s_xq = sem()
+    A.wait_ge(ld, 16)
+    for q in range(4):
+        A.activation(blk(T.xq, q), T.xs[:, q:512:4], COPY).then_inc(s_xq, 1)
 
     s_pt, s_xt = sem(), sem()
     P.wait_ge(c_id, 1)
@@ -147,18 +135,22 @@ def rank_program(g, core, T, topo):
     V.wait_ge(s_ps, 4)
     V.reciprocal(T.u1[:], T.ps[:, 0:1]).then_inc(s_u1, 1)
     P.wait_ge(s_u1, 1)
+    P.wait_ge(s_xq, 4)
     for q in range(4):
-        P.matmul(T.pc2[:, q:q + 1], blk(T.xs, q), T.u1[:], True, True).then_inc(s_pc2, 1)
+        P.matmul(T.pc2[:, q:q + 1], blk(T.xq, q), T.u1[:], True, True).then_inc(s_pc2, 1)
     V.wait_ge(s_pc2, 4)
     V.tensor_copy(blk(T.land2, me, 4), T.pc2[:, 0:4]).then_inc(s_part2, 1)
     g.wait_ge(s_part2, 1)
     send_part(T.land2, T.sem.arr2)
 
-    s_xu, s_zu = sem(), sem()
+    s_pu, s_zq = sem(), sem()
+    Z = [T.z0, T.z1, T.z2, T.z3]
     A.wait_ge(s_u1, 1)
-    A.activation(T.xu[:], T.xs[:], COPY, scale=T.u1[:, 0:1]).then_inc(s_xu, 1)
-    V.wait_ge(s_xu, 1)
-    V.transpose(T.zu[:], T.xu[:]).then_inc(s_zu, 1)
+    A.wait_ge(c_perm, 1)
+    A.activation(T.pu[:], T.pmat[:], COPY, scale=T.u1[:, 0:1]).then_inc(s_pu, 1)
+    P.wait_ge(s_pu, 1)
+    for q in range(4):
+        P.matmul(Z[q][:, 0:128], blk(T.xq, q), T.pu[:], True, True).then_inc(s_zq, 1)
 
     if is_hub:
         s_t, n_t = hub_sum(T.land2, s_part2, T.t4, T.sem.arr2), 4
@@ -167,54 +159,43 @@ def rank_program(g, core, T, topo):
     else:
         s_t, n_t = T.sem.res2, engines(my_hub, core)
 
-    s_tm, s_pw, s_wv = sem(), sem(), sem()
-    V.wait_ge(m1, 4)
+    s_v = sem()
     V.wait_ge(s_t, n_t)
-    A.wait_ge(m1, 4)
-    A.wait_ge(s_t, n_t)
-    for a in range(2):
-        V.tensor_scalar(blk(T.tm, a, 4), T.t4[:], T.ind[:, a:a + 1], None, MUL).then_inc(s_tm, 1)
-    for a in range(2, 4):
-        A.activation(blk(T.tm, a, 4), T.t4[:], COPY, scale=T.ind[:, a:a + 1]).then_inc(s_tm, 1)
-    P.wait_ge(c_r, 1)
-    P.wait_ge(s_tm, 4)
-    P.matmul(T.pw[:, 0:16], T.rmat[:], T.tm[:], True, True).then_inc(s_pw, 1)
-    V.wait_ge(s_pw, 1)
-    V.reciprocal(T.wv[:], T.pw[:, 0:16]).then_inc(s_wv, 1)
-
-    def col(b):
-        c = 4 * (b % 4) + b // 4
-        return T.wv[:, c:c + 1]
-
-    s_z = [sem() for _ in range(4)]
+    V.reciprocal(T.v4[:], T.t4[:]).then_inc(s_v, 1)
+    s_s = [[sem() for _ in range(2)] for _ in range(4)]
     s_y = [sem() for _ in range(2)]
-    st = sem()
-    A.wait_ge(s_wv, 1)
-    A.wait_ge(s_zu, 1)
-    for b in range(16):
-        if b % 4 != 3:
-            A.activation(blk(T.zs, b, 32), blk(T.zu, b, 32), COPY, scale=col(b)).then_inc(s_z[b // 4], 1)
+    st_s, st_a = sem(), sem()
 
-    def vscale(q):
-        b = 4 * q + 3
-        V.tensor_scalar(blk(T.zs, b, 32), blk(T.zu, b, 32), col(b), None, MUL).then_inc(s_z[q], 1)
+    def zin(q, h):
+        return Z[q][:, 64 * h:64 * h + 64]
 
-    def vback(q):
-        V.wait_ge(s_z[q], 4)
-        V.transpose(blk(T.ys, q), blk(T.zs, q)).then_inc(s_y[q // 2], 1)
+    def zout(q, h):
+        return T.zs[:, 128 * q + 64 * h:128 * q + 64 * h + 64]
 
-    V.wait_ge(s_wv, 1)
-    V.wait_ge(s_zu, 1)
-    vscale(0)
-    vscale(1)
-    vback(0)
-    vscale(2)
-    vback(1)
-    vscale(3)
-    vback(2)
-    vback(3)
+    A.wait_ge(s_v, 1)
+    A.wait_ge(s_zq, 4)
     for h in range(2):
-        S.wait_ge(s_y[h], 2)
-        S.dma_start(T.y[:, 256 * h:256 * h + 256], T.ys[:, 256 * h:256 * h + 256]).then_inc(st, 16)
-    S.wait_ge(st, 32)
+        for q in range(3):
+            A.activation(zout(q, h), zin(q, h), COPY, scale=T.v4[:, q:q + 1]).then_inc(s_s[q][h], 1)
+    V.wait_ge(s_v, 1)
+    V.wait_ge(s_zq, 4)
+    for h in range(2):
+        V.tensor_scalar(zout(3, h), zin(3, h), T.v4[:, 3:4], None, MUL).then_inc(s_s[3][h], 1)
+    for h in range(2):
+        for q in range(4):
+            V.wait_ge(s_s[q][h], 1)
+            V.transpose(T.ys[:, 256 * h + q:256 * h + 256:4], zout(q, h)).then_inc(s_y[h], 1)
+
+    def store(Q, st, a, h):
+        Q.dma_start(T.y[64 * h:64 * h + 64, 128 * a:128 * a + 128],
+                    T.ys[32 * a:32 * a + 32, 256 * h:256 * h + 256]).then_inc(st, 16)
+
+    for h in range(2):
+        S.wait_ge(s_y[h], 4)
+        A.wait_ge(s_y[h], 4)
+        for a in range(2):
+            store(S, st_s, a, h)
+            store(A, st_a, a + 2, h)
+    S.wait_ge(st_s, 64)
+    A.wait_ge(st_a, 64)
     g.wait_ge(T.sem.sent, sent[0])

from concourse.bass import DstId, RemoteDMATransfer
from concourse.mybir import AluOpType, AxisListType, ActivationFunctionType

F = "float32"
NR = 9
SCRATCH = {
    "xs": ("sbuf", [128, 512], F), "xt": ("sbuf", [128, 512], F), "xq": ("sbuf", [128, 512], F),
    "zs": ("sbuf", [128, 512], F), "ys": ("sbuf", [128, 512], F), "sc": ("sbuf", [128, 256], F),
    "ones": ("sbuf", [128, 128], F), "ident": ("sbuf", [128, 128], F), "pmat": ("sbuf", [128, 128], F),
    "pu": ("sbuf", [128, 128], F),
    "r1": ("sbuf", [128, 1], F),
    "land1": ("sbuf", [128, 4 * NR], F), "c1": ("sbuf", [128, 4], F), "w1": ("sbuf", [128, 4], F),
    "u1": ("sbuf", [128, 1], F),
    "land2": ("sbuf", [128, 4 * NR], F), "t4": ("sbuf", [128, 4], F), "v4": ("sbuf", [128, 4], F),
    "pc1": ("psum", [128, 512], F), "pt": ("psum", [128, 512], F), "ps": ("psum", [128, 512], F),
    "pc2": ("psum", [128, 512], F),
    "z0": ("psum", [128, 512], F), "z1": ("psum", [128, 512], F), "z2": ("psum", [128, 512], F),
    "z3": ("psum", [128, 512], F),
}
NLOCAL = 48
SEMAPHORES = ["arr1", "res1", "arr2", "res2", "sent"] + ["l%d" % i for i in range(NLOCAL)]

ADD, MUL = AluOpType.add, AluOpType.mult
COPY = ActivationFunctionType.Copy


def _plan(cores, topo):
    hubs = [c for c in cores if all(topo.may_write(c, d) and topo.may_write(d, c) for d in cores if d != c)]
    leaves = [c for c in cores if c not in hubs]
    served = {h: [] for h in hubs}
    for l in leaves:
        h = sorted(hubs, key=lambda k: (len(served[k]), topo.chip(k) != topo.chip(l)))[0]
        served[h].append(l)
    return hubs, leaves, served


def rank_program(g, core, T, topo):
    if T.rank_of(core) is None:
        return
    cores = list(T.cores)
    hubs, leaves, served = _plan(cores, topo)
    is_hub = core in hubs
    me = cores.index(core)
    V, A, P, S = g.vector, g.scalar, g.tensor, g.sync
    used = [0]
    sent = [0]

    def sem():
        used[0] += 1
        return T.sem["l%d" % (used[0] - 1)]

    def blk(t, q, w=128):
        return t[:, q * w:(q + 1) * w]

    def send(src, dests, dst_aps, rsem):
        m = topo.mask(core, dests[0])
        for d in dests:
            m &= topo.mask(core, d)
        ids = []
        for d in dests:
            rid, pid = topo.addr(d, core)
            ids.append(DstId(rid=rid, pnc=pid))
        g.remote_dma_fused([RemoteDMATransfer(dst_ids=ids, dma_engine_mask=m, remote_sem=rsem, srcs=[src],
                                              dsts=dst_aps, alu_op=0)], local_sem=T.sem.sent)
        sent[0] += bin(m).count("1")

    def engines(src, dst):
        return bin(topo.mask(src, dst)).count("1")

    n_in = sum(engines(c, core) for c in cores if c != core)

    def send_part(land, arr):
        dests = [h for h in hubs if h != core]
        send(blk(land, me, 4), dests, [blk(land, me, 4)] * len(dests), arr)

    def hub_sum(land, s_part, out, arr):
        sd = sem()
        V.wait_ge(s_part, 1)
        V.wait_ge(arr, n_in)
        for q in range(4):
            V.tensor_reduce(out[:, q:q + 1], land[:, q:4 * NR:4], AxisListType.X, ADD).then_inc(sd, 1)
        return sd

    ld = sem()
    S.dma_start(T.xs[:], T.x[:]).then_inc(ld, 16)
    c_ones, c_id, c_perm = sem(), sem(), sem()
    V.memset(T.ones[:], 1.0).then_inc(c_ones, 1)
    g.wait_ge(c_ones, 1)
    g.affine_select(T.ident[:], T.ones[:], [[-1, 128]], AluOpType.is_equal, 0.0, 0, 1).then_inc(c_id, 1)
    g.affine_select(T.pmat[:], T.ones[:], [[-64, 2], [-1, 2], [-2, 32]], AluOpType.is_equal, 0.0, 0,
                    1).then_inc(c_perm, 1)

    s_rs, s_r1, s_pc1, s_part1 = sem(), sem(), sem(), sem()
    V.wait_ge(ld, 16)
    V.tensor_tensor_scan(T.sc[:], T.xs[:, 0:256], T.xs[:, 256:512], 0.0, ADD, ADD).then_inc(s_rs, 1)
    V.wait_ge(s_rs, 1)
    V.reciprocal(T.r1[:], T.sc[:, 255:256]).then_inc(s_r1, 1)
    P.wait_ge(ld, 16)
    P.wait_ge(s_r1, 1)
    for q in range(4):
        P.matmul(T.pc1[:, q:q + 1], blk(T.xs, q), T.r1[:], True, True).then_inc(s_pc1, 1)
    V.wait_ge(s_pc1, 4)
    V.tensor_copy(blk(T.land1, me, 4), T.pc1[:, 0:4]).then_inc(s_part1, 1)
    g.wait_ge(s_part1, 1)
    send_part(T.land1, T.sem.arr1)

    s_xq = sem()
    A.wait_ge(ld, 16)
    for q in range(4):
        A.activation(blk(T.xq, q), T.xs[:, q:512:4], COPY).then_inc(s_xq, 1)

    s_pt, s_xt = sem(), sem()
    P.wait_ge(c_id, 1)
    for q in range(4):
        P.transpose(blk(T.pt, q), blk(T.xs, q), T.ident[:]).then_inc(s_pt, 1)
    A.wait_ge(s_pt, 4)
    A.activation(T.xt[:], T.pt[:], COPY).then_inc(s_xt, 1)

    if is_hub:
        s_c1 = hub_sum(T.land1, s_part1, T.c1, T.sem.arr1)
        s_w1, n_w1 = sem(), 1
        V.wait_ge(s_c1, 4)
        V.reciprocal(T.w1[:], T.c1[:]).then_inc(s_w1, 1)
        g.wait_ge(s_w1, 1)
        send(T.w1[:], served[core], [T.w1[:]] * len(served[core]), T.sem.res1)
    else:
        my_hub = [h for h in hubs if core in served[h]][0]
        s_w1, n_w1 = T.sem.res1, engines(my_hub, core)

    s_ps, s_u1, s_pc2, s_part2 = sem(), sem(), sem(), sem()
    P.wait_ge(s_w1, n_w1)
    P.wait_ge(s_xt, 1)
    for q in range(4):
        P.matmul(T.ps[:, 0:1], blk(T.xt, q), T.w1[:, q:q + 1], q == 0, q == 3).then_inc(s_ps, 1)
    V.wait_ge(s_ps, 4)
    V.reciprocal(T.u1[:], T.ps[:, 0:1]).then_inc(s_u1, 1)
    P.wait_ge(s_u1, 1)
    P.wait_ge(s_xq, 4)
    for q in range(4):
        P.matmul(T.pc2[:, q:q + 1], blk(T.xq, q), T.u1[:], True, True).then_inc(s_pc2, 1)
    V.wait_ge(s_pc2, 4)
    V.tensor_copy(blk(T.land2, me, 4), T.pc2[:, 0:4]).then_inc(s_part2, 1)
    g.wait_ge(s_part2, 1)
    send_part(T.land2, T.sem.arr2)

    s_pu, s_zq = sem(), sem()
    Z = [T.z0, T.z1, T.z2, T.z3]
    A.wait_ge(s_u1, 1)
    A.wait_ge(c_perm, 1)
    A.activation(T.pu[:], T.pmat[:], COPY, scale=T.u1[:, 0:1]).then_inc(s_pu, 1)
    P.wait_ge(s_pu, 1)
    for q in range(4):
        P.matmul(Z[q][:, 0:128], blk(T.xq, q), T.pu[:], True, True).then_inc(s_zq, 1)

    if is_hub:
        s_t, n_t = hub_sum(T.land2, s_part2, T.t4, T.sem.arr2), 4
        g.wait_ge(s_t, n_t)
        send(T.t4[:], served[core], [T.t4[:]] * len(served[core]), T.sem.res2)
    else:
        s_t, n_t = T.sem.res2, engines(my_hub, core)

    s_v = sem()
    V.wait_ge(s_t, n_t)
    V.reciprocal(T.v4[:], T.t4[:]).then_inc(s_v, 1)
    s_s = [[sem() for _ in range(2)] for _ in range(4)]
    s_y = [sem() for _ in range(2)]
    st_s, st_a = sem(), sem()

    def zin(q, h):
        return Z[q][:, 64 * h:64 * h + 64]

    def zout(q, h):
        return T.zs[:, 128 * q + 64 * h:128 * q + 64 * h + 64]

    A.wait_ge(s_v, 1)
    A.wait_ge(s_zq, 4)
    for h in range(2):
        for q in range(3):
            A.activation(zout(q, h), zin(q, h), COPY, scale=T.v4[:, q:q + 1]).then_inc(s_s[q][h], 1)
    V.wait_ge(s_v, 1)
    V.wait_ge(s_zq, 4)
    for h in range(2):
        V.tensor_scalar(zout(3, h), zin(3, h), T.v4[:, 3:4], None, MUL).then_inc(s_s[3][h], 1)
    for h in range(2):
        for q in range(4):
            V.wait_ge(s_s[q][h], 1)
            V.transpose(T.ys[:, 256 * h + q:256 * h + 256:4], zout(q, h)).then_inc(s_y[h], 1)

    def store(Q, st, a, h):
        Q.dma_start(T.y[64 * h:64 * h + 64, 128 * a:128 * a + 128],
                    T.ys[32 * a:32 * a + 32, 256 * h:256 * h + 256]).then_inc(st, 16)

    for h in range(2):
        S.wait_ge(s_y[h], 4)
        A.wait_ge(s_y[h], 4)
        for a in range(2):
            store(S, st_s, a, h)
            store(A, st_a, a + 2, h)
    S.wait_ge(st_s, 64)
    A.wait_ge(st_a, 64)
    g.wait_ge(T.sem.sent, sent[0])
